import numpy as np, ml_dtypes
CORES = [50,106,114,52,108,116]
N = 6
GR, GC, TK = 2, 3, 128
RA = [[1,1],[-2,-2]]
CB = [[-2,-2,-2],[-2,2,-1],[-2,-2,1]]
def setup_inputs(rng):
    return {"x": rng.standard_normal((N, 128, TK), dtype=np.float32).astype(ml_dtypes.bfloat16), "a": (rng.standard_normal((N, 128, 128), dtype=np.float32) / 11).astype(ml_dtypes.bfloat16)}
def setup_inputs_big(rng):
    d = setup_inputs(rng)
    for k in ("x", "a"): d[k] = (d[k].astype(np.float32) * 1024.0).astype(d[k].dtype)
    return d
def setup_inputs_small(rng):
    d = setup_inputs(rng)
    for k in ("x", "a"): d[k] = (d[k].astype(np.float32) * (1 / 1024.0)).astype(d[k].dtype)
    return d
def setup_inputs_apart(rng):
    d = setup_inputs(rng)
    f = (10.0 ** rng.permutation(np.linspace(-1.5, 1.5, N))).astype(np.float32).reshape(N, 1, 1)
    for k in ("x", "a"): d[k] = (d[k].astype(np.float32) * f).astype(d[k].dtype)
    return d
def reference(x, a):
    X, A = x.astype(np.float64), a.astype(np.float64)
    y = np.zeros((N, 128, TK))
    for i in range(GR):
        for j in range(GC):
            t = sum(RA[i][k] * CB[j][l] * X[k * GC + l] for k in range(GR) for l in range(GC))
            y[i * GC + j] = A[i * GC + j].T @ t
    return {"y": y.astype(ml_dtypes.bfloat16)}

@@ -1,0 +1,132 @@
+from concourse.bass import DstId, RemoteDMATransfer
+from concourse.mybir import AluOpType
+
+GR, GC = 2, 3
+NE = 8
+
+SCRATCH = {
+    "xs": ("sbuf", [128, 128], "bfloat16"),
+    "aa": ("sbuf", [128, 128], "bfloat16"),
+    "ys": ("sbuf", [128, 128], "bfloat16"),
+    "acc": ("psum", [128, 128], "float32"),
+}
+for _k in range(GR):
+    SCRATCH["p%d" % _k] = ("sbuf", [128, 128], "bfloat16")
+for _l in range(GC):
+    SCRATCH["s%d" % _l] = ("sbuf", [128, 128], "bfloat16")
+    SCRATCH["k%d" % _l] = ("sbuf", [128, 128], "bfloat16")
+    SCRATCH["w%d" % _l] = ("sbuf", [128, 128], "bfloat16")
+
+SEMAPHORES = (["xl", "al", "sent", "cs", "sc", "mm", "cp", "st"]
+              + ["p%d" % _k for _k in range(GR)] + ["s%d" % _l for _l in range(GC)])
+
+
+def _bits(mask):
+    n = 0
+    while mask:
+        n += mask & 1
+        mask >>= 1
+    return n
+
+
+def _lowest(mask, n):
+    out, b = 0, 1
+    while n:
+        if mask & b:
+            out |= b
+            n -= 1
+        b <<= 1
+    return out
+
+
+def _plan(T, topo):
+    col = [[T.cores[k * GC + l] for k in range(GR)] for l in range(GC)]
+    out, src, eng = {}, {}, {}
+    for l in range(GC):
+        assert all(topo.chip(c) == topo.chip(col[l][0]) for c in col[l])
+        for c in col[l]:
+            out[c] = []
+        may = {m: [c for c in col[l] if all(topo.may_write(c, d) for d in col[m])] for m in range(GC) if m != l}
+        for m in sorted(may, key=lambda q: len(may[q])):
+            c = min(may[m], key=lambda q: len(out[q]))
+            out[c].append(m)
+            src[(l, m)] = c
+        for c in col[l]:
+            mask = None
+            for d in [p for p in col[l] if p != c] + [d for m in out[c] for d in col[m]]:
+                mask = topo.mask(c, d) if mask is None else mask & topo.mask(c, d)
+            eng[c] = _lowest(mask, min(NE, _bits(mask)))
+    return col, out, src, eng
+
+
+def _dst(topo, c):
+    rid, pid, _ = topo.addr(c)
+    return DstId(rid=rid, pnc=pid)
+
+
+def rank_program(g, core, T, topo):
+    rank = T.rank_of(core)
+    if rank is None:
+        return
+    RA, CB = T.tables["RA"], T.tables["CB"]
+    assert all(v == row[0] for row in RA for v in row)
+    i, j = rank // GC, rank % GC
+    col, out, src, eng = _plan(T, topo)
+    S = T.sem
+    mates_on_chip = [k for k in range(GR) if k != i]
+
+    g.sync.dma_start(T.xs[:], T.x[:]).then_inc(S.xl, 16)
+    g.scalar.wait_ge(S.xl, 16)
+    g.scalar.dma_start(T.aa[:], T.a[:]).then_inc(S.al, 16)
+
+    sent = 0
+    g.wait_ge(S.xl, 16)
+    g.remote_dma_fused(
+        [RemoteDMATransfer(dst_ids=[_dst(topo, col[j][k]) for k in mates_on_chip], dma_engine_mask=eng[core],
+                           remote_sem=S["p%d" % i], srcs=[T.xs[:]], dsts=[T["p%d" % i][:] for _ in mates_on_chip],
+                           alu_op=0)],
+        local_sem=S.sent)
+    sent += _bits(eng[core])
+    if out[core]:
+        for k in mates_on_chip:
+            g.wait_ge(S["p%d" % k], _bits(eng[col[j][k]]))
+        far = [d for m in out[core] for d in col[m]]
+        g.remote_dma_fused(
+            [RemoteDMATransfer(dst_ids=[_dst(topo, d) for d in far], dma_engine_mask=eng[core],
+                               remote_sem=S["s%d" % j], srcs=[T.xs[:]] + [T["p%d" % k][:] for k in mates_on_chip],
+                               dsts=[T["s%d" % j][:] for _ in far], alu_op=1)],
+            local_sem=S.sent)
+        sent += _bits(eng[core])
+    g.wait_ge(S.sent, sent)
+
+    weight = [RA[i][0] * CB[j][l] for l in range(GC)]
+    vals = sorted(set(w for w in weight if w != 1))
+    lhs = {1: T.aa}
+    for n, w in enumerate(vals):
+        g.vector.memset(T["k%d" % n][:], float(w)).then_inc(S.cs, 1)
+        lhs[w] = T["w%d" % n]
+    if vals:
+        g.vector.wait_ge(S.cs, len(vals))
+    g.vector.wait_ge(S.al, 16)
+    for n, w in enumerate(vals):
+        g.vector.tensor_tensor(T["w%d" % n][:], T.aa[:], T["k%d" % n][:], AluOpType.mult).then_inc(S.sc, 1)
+
+    g.tensor.wait_ge(S.al, 16)
+    if vals:
+        g.tensor.wait_ge(S.sc, len(vals))
+    g.tensor.wait_ge(S.xl, 16)
+    g.tensor.matmul(T.acc[:], lhs[weight[j]][:], T.xs[:], True, False)
+    for k in mates_on_chip:
+        g.tensor.wait_ge(S["p%d" % k], _bits(eng[col[j][k]]))
+        g.tensor.matmul(T.acc[:], lhs[weight[j]][:], T["p%d" % k][:], False, False)
+    others = sorted((l for l in range(GC) if l != j), key=lambda l: len(out[src[(l, j)]]))
+    for n, l in enumerate(others):
+        g.tensor.wait_ge(S["s%d" % l], _bits(eng[src[(l, j)]]))
+        mm = g.tensor.matmul(T.acc[:], lhs[weight[l]][:], T["s%d" % l][:], False, n == len(others) - 1)
+    mm.then_inc(S.mm, 1)
+
+    g.vector.wait_ge(S.mm, 1)
+    g.vector.tensor_copy(T.ys[:], T.acc[:]).then_inc(S.cp, 1)
+    g.sync.wait_ge(S.cp, 1)
+    g.sync.dma_start(T.y[:], T.ys[:]).then_inc(S.st, 16)
+    g.sync.wait_ge(S.st, 16)

@@ -5,20 +5,22 @@ GR, GC = 2, 3
 NE = 8
 
 SCRATCH = {
+    "xd": ("dram", [128, 128], "bfloat16"),
     "xs": ("sbuf", [128, 128], "bfloat16"),
     "aa": ("sbuf", [128, 128], "bfloat16"),
     "ys": ("sbuf", [128, 128], "bfloat16"),
     "acc": ("psum", [128, 128], "float32"),
 }
 for _k in range(GR):
+    SCRATCH["pd%d" % _k] = ("dram", [128, 128], "bfloat16")
     SCRATCH["p%d" % _k] = ("sbuf", [128, 128], "bfloat16")
 for _l in range(GC):
     SCRATCH["s%d" % _l] = ("sbuf", [128, 128], "bfloat16")
     SCRATCH["k%d" % _l] = ("sbuf", [128, 128], "bfloat16")
     SCRATCH["w%d" % _l] = ("sbuf", [128, 128], "bfloat16")
 
-SEMAPHORES = (["xl", "al", "sent", "cs", "sc", "mm", "cp", "st"]
-              + ["p%d" % _k for _k in range(GR)] + ["s%d" % _l for _l in range(GC)])
+SEMAPHORES = (["xl", "xm", "al", "sent", "cs", "sc", "mm", "cp", "st"]
+              + ["q%d" % _k for _k in range(GR)] + ["p%d" % _k for _k in range(GR)] + ["s%d" % _l for _l in range(GC)])
 
 
 def _bits(mask):
@@ -29,7 +31,14 @@ def _bits(mask):
     return n
 
 
-def _lowest(mask, n):
+def _engines(topo, c, dsts, n, avoid=0):
+    mask = None
+    for d in dsts:
+        mask = topo.mask(c, d) if mask is None else mask & topo.mask(c, d)
+    if mask is None:
+        return 0
+    mask &= ~avoid
+    n = min(n, _bits(mask))
     out, b = 0, 1
     while n:
         if mask & b:
@@ -41,22 +50,37 @@ def _lowest(mask, n):
 
 def _plan(T, topo):
     col = [[T.cores[k * GC + l] for k in range(GR)] for l in range(GC)]
-    out, src, eng = {}, {}, {}
+    aid, out, src, d1, e1, e2, e3 = {}, {}, {}, {}, {}, {}, {}
     for l in range(GC):
-        assert all(topo.chip(c) == topo.chip(col[l][0]) for c in col[l])
+        here = topo.chip(col[l][0])
+        assert all(topo.chip(c) == here for c in col[l])
+        far = [m for m in range(GC) if m != l]
         for c in col[l]:
             out[c] = []
-        may = {m: [c for c in col[l] if all(topo.may_write(c, d) for d in col[m])] for m in range(GC) if m != l}
+        may = {m: [c for c in col[l] if all(topo.may_write(c, d) for d in col[m])] for m in far}
         for m in sorted(may, key=lambda q: len(may[q])):
             c = min(may[m], key=lambda q: len(out[q]))
-            out[c].append(m)
-            src[(l, m)] = c
-        for c in col[l]:
-            mask = None
-            for d in [p for p in col[l] if p != c] + [d for m in out[c] for d in col[m]]:
-                mask = topo.mask(c, d) if mask is None else mask & topo.mask(c, d)
-            eng[c] = _lowest(mask, min(NE, _bits(mask)))
-    return col, out, src, eng
+            out[c] = out[c] + col[m]
+        senders = [c for c in col[l] if out[c]]
+        aid[l] = []
+        if len(senders) < len(far):
+            busy = max(senders, key=lambda q: len(out[q]))
+            dies = [topo.die(c) for c in senders]
+            spare = [c for c in range(topo.CHIPS * topo.CORES_PER_CHIP)
+                     if topo.chip(c) == here and T.rank_of(c) is None and all(topo.may_write(c, d) for d in out[busy])]
+            h = min(spare, key=lambda q: (dies.count(topo.die(q)), q))
+            d = max(out[busy], key=lambda q: (topo.die(q) == topo.die(h), q))
+            out[busy] = [q for q in out[busy] if q != d]
+            out[h] = [d]
+            aid[l] = [h]
+        for c in col[l] + aid[l]:
+            for d in out[c]:
+                src[(l, d)] = c
+            d1[c] = aid[l] + [p for p in senders if p != c] if c in col[l] else []
+            e1[c] = _engines(topo, c, d1[c], NE)
+            e2[c] = _engines(topo, c, out[c], NE)
+            e3[c] = _engines(topo, c, [p for p in col[l] if p != c] if c in col[l] else [], NE, e1[c] | e2[c])
+    return col, aid, out, src, d1, e1, e2, e3
 
 
 def _dst(topo, c):
@@ -64,40 +88,51 @@ def _dst(topo, c):
     return DstId(rid=rid, pnc=pid)
 
 
+def _copy(g, T, topo, tile, dsts, name, sem, mask):
+    g.remote_dma_fused(
+        [RemoteDMATransfer(dst_ids=[_dst(topo, d) for d in dsts], dma_engine_mask=mask, remote_sem=T.sem[sem],
+                           srcs=[tile], dsts=[T[name][:] for _ in dsts], alu_op=0)],
+        local_sem=T.sem.sent)
+
+
+def _fold_and_send(g, T, topo, core, l, tiles, out, e2):
+    g.remote_dma_fused(
+        [RemoteDMATransfer(dst_ids=[_dst(topo, d) for d in out[core]], dma_engine_mask=e2[core],
+                           remote_sem=T.sem["s%d" % l], srcs=tiles, dsts=[T["s%d" % l][:] for _ in out[core]],
+                           alu_op=1)],
+        local_sem=T.sem.sent)
+
+
 def rank_program(g, core, T, topo):
+    col, aid, out, src, d1, e1, e2, e3 = _plan(T, topo)
+    S = T.sem
     rank = T.rank_of(core)
     if rank is None:
+        for l in range(GC):
+            if core in aid[l]:
+                for k in range(GR):
+                    g.wait_ge(S["q%d" % k], _bits(e1[col[l][k]]))
+                _fold_and_send(g, T, topo, core, l, [T["pd%d" % k][:] for k in range(GR)], out, e2)
+                g.wait_ge(S.sent, _bits(e2[core]))
         return
     RA, CB = T.tables["RA"], T.tables["CB"]
     assert all(v == row[0] for row in RA for v in row)
     i, j = rank // GC, rank % GC
-    col, out, src, eng = _plan(T, topo)
-    S = T.sem
     mates_on_chip = [k for k in range(GR) if k != i]
 
-    g.sync.dma_start(T.xs[:], T.x[:]).then_inc(S.xl, 16)
-    g.scalar.wait_ge(S.xl, 16)
-    g.scalar.dma_start(T.aa[:], T.a[:]).then_inc(S.al, 16)
+    g.sync.dma_start(T.xd[:], T.x[:]).then_inc(S.xl, 16)
+    g.sync.dma_start(T.xs[:], T.x[:]).then_inc(S.xm, 16)
+    g.sync.dma_start(T.aa[:], T.a[:]).then_inc(S.al, 16)
 
-    sent = 0
     g.wait_ge(S.xl, 16)
-    g.remote_dma_fused(
-        [RemoteDMATransfer(dst_ids=[_dst(topo, col[j][k]) for k in mates_on_chip], dma_engine_mask=eng[core],
-                           remote_sem=S["p%d" % i], srcs=[T.xs[:]], dsts=[T["p%d" % i][:] for _ in mates_on_chip],
-                           alu_op=0)],
-        local_sem=S.sent)
-    sent += _bits(eng[core])
+    if d1[core]:
+        _copy(g, T, topo, T.xd[:], d1[core], "pd%d" % i, "q%d" % i, e1[core])
     if out[core]:
         for k in mates_on_chip:
-            g.wait_ge(S["p%d" % k], _bits(eng[col[j][k]]))
-        far = [d for m in out[core] for d in col[m]]
-        g.remote_dma_fused(
-            [RemoteDMATransfer(dst_ids=[_dst(topo, d) for d in far], dma_engine_mask=eng[core],
-                               remote_sem=S["s%d" % j], srcs=[T.xs[:]] + [T["p%d" % k][:] for k in mates_on_chip],
-                               dsts=[T["s%d" % j][:] for _ in far], alu_op=1)],
-            local_sem=S.sent)
-        sent += _bits(eng[core])
-    g.wait_ge(S.sent, sent)
+            g.wait_ge(S["q%d" % k], _bits(e1[col[j][k]]))
+        _fold_and_send(g, T, topo, core, j, [T.xd[:]] + [T["pd%d" % k][:] for k in mates_on_chip], out, e2)
+    _copy(g, T, topo, T.xd[:], [col[j][k] for k in mates_on_chip], "p%d" % i, "p%d" % i, e3[core])
+    g.wait_ge(S.sent, _bits(e1[core]) + _bits(e2[core]) + _bits(e3[core]))
 
     weight = [RA[i][0] * CB[j][l] for l in range(GC)]
     vals = sorted(set(w for w in weight if w != 1))
@@ -114,14 +149,15 @@ def rank_program(g, core, T, topo):
     g.tensor.wait_ge(S.al, 16)
     if vals:
         g.tensor.wait_ge(S.sc, len(vals))
-    g.tensor.wait_ge(S.xl, 16)
+    g.tensor.wait_ge(S.xm, 16)
     g.tensor.matmul(T.acc[:], lhs[weight[j]][:], T.xs[:], True, False)
-    for k in mates_on_chip:
-        g.tensor.wait_ge(S["p%d" % k], _bits(eng[col[j][k]]))
-        g.tensor.matmul(T.acc[:], lhs[weight[j]][:], T["p%d" % k][:], False, False)
-    others = sorted((l for l in range(GC) if l != j), key=lambda l: len(out[src[(l, j)]]))
+    others = sorted((l for l in range(GC) if l != j), key=lambda l: len(aid[l]))
     for n, l in enumerate(others):
-        g.tensor.wait_ge(S["s%d" % l], _bits(eng[src[(l, j)]]))
+        if n == len(others) - 1:
+            for k in mates_on_chip:
+                g.tensor.wait_ge(S["p%d" % k], _bits(e3[col[j][k]]))
+                g.tensor.matmul(T.acc[:], lhs[weight[j]][:], T["p%d" % k][:], False, False)
+        g.tensor.wait_ge(S["s%d" % l], _bits(e2[src[(l, core)]]))
         mm = g.tensor.matmul(T.acc[:], lhs[weight[l]][:], T["s%d" % l][:], False, n == len(others) - 1)
     mm.then_inc(S.mm, 1)
 

from concourse.bass import DstId, RemoteDMATransfer
from concourse.mybir import AluOpType

GR, GC = 2, 3
NE = 8

SCRATCH = {
    "xd": ("dram", [128, 128], "bfloat16"),
    "xs": ("sbuf", [128, 128], "bfloat16"),
    "aa": ("sbuf", [128, 128], "bfloat16"),
    "ys": ("sbuf", [128, 128], "bfloat16"),
    "acc": ("psum", [128, 128], "float32"),
}
for _k in range(GR):
    SCRATCH["pd%d" % _k] = ("dram", [128, 128], "bfloat16")
    SCRATCH["p%d" % _k] = ("sbuf", [128, 128], "bfloat16")
for _l in range(GC):
    SCRATCH["s%d" % _l] = ("sbuf", [128, 128], "bfloat16")
    SCRATCH["k%d" % _l] = ("sbuf", [128, 128], "bfloat16")
    SCRATCH["w%d" % _l] = ("sbuf", [128, 128], "bfloat16")

SEMAPHORES = (["xl", "xm", "al", "sent", "cs", "sc", "mm", "cp", "st"]
              + ["q%d" % _k for _k in range(GR)] + ["p%d" % _k for _k in range(GR)] + ["s%d" % _l for _l in range(GC)])


def _bits(mask):
    n = 0
    while mask:
        n += mask & 1
        mask >>= 1
    return n


def _engines(topo, c, dsts, n, avoid=0):
    mask = None
    for d in dsts:
        mask = topo.mask(c, d) if mask is None else mask & topo.mask(c, d)
    if mask is None:
        return 0
    mask &= ~avoid
    n = min(n, _bits(mask))
    out, b = 0, 1
    while n:
        if mask & b:
            out |= b
            n -= 1
        b <<= 1
    return out


def _plan(T, topo):
    col = [[T.cores[k * GC + l] for k in range(GR)] for l in range(GC)]
    aid, out, src, d1, e1, e2, e3 = {}, {}, {}, {}, {}, {}, {}
    for l in range(GC):
        here = topo.chip(col[l][0])
        assert all(topo.chip(c) == here for c in col[l])
        far = [m for m in range(GC) if m != l]
        for c in col[l]:
            out[c] = []
        may = {m: [c for c in col[l] if all(topo.may_write(c, d) for d in col[m])] for m in far}
        for m in sorted(may, key=lambda q: len(may[q])):
            c = min(may[m], key=lambda q: len(out[q]))
            out[c] = out[c] + col[m]
        senders = [c for c in col[l] if out[c]]
        aid[l] = []
        if len(senders) < len(far):
            busy = max(senders, key=lambda q: len(out[q]))
            dies = [topo.die(c) for c in senders]
            spare = [c for c in range(topo.CHIPS * topo.CORES_PER_CHIP)
                     if topo.chip(c) == here and T.rank_of(c) is None and all(topo.may_write(c, d) for d in out[busy])]
            h = min(spare, key=lambda q: (dies.count(topo.die(q)), q))
            d = max(out[busy], key=lambda q: (topo.die(q) == topo.die(h), q))
            out[busy] = [q for q in out[busy] if q != d]
            out[h] = [d]
            aid[l] = [h]
        for c in col[l] + aid[l]:
            for d in out[c]:
                src[(l, d)] = c
            d1[c] = aid[l] + [p for p in senders if p != c] if c in col[l] else []
            e1[c] = _engines(topo, c, d1[c], NE)
            e2[c] = _engines(topo, c, out[c], NE)
            e3[c] = _engines(topo, c, [p for p in col[l] if p != c] if c in col[l] else [], NE, e1[c] | e2[c])
    return col, aid, out, src, d1, e1, e2, e3


def _dst(topo, c):
    rid, pid, _ = topo.addr(c)
    return DstId(rid=rid, pnc=pid)


def _copy(g, T, topo, tile, dsts, name, sem, mask):
    g.remote_dma_fused(
        [RemoteDMATransfer(dst_ids=[_dst(topo, d) for d in dsts], dma_engine_mask=mask, remote_sem=T.sem[sem],
                           srcs=[tile], dsts=[T[name][:] for _ in dsts], alu_op=0)],
        local_sem=T.sem.sent)


def _fold_and_send(g, T, topo, core, l, tiles, out, e2):
    g.remote_dma_fused(
        [RemoteDMATransfer(dst_ids=[_dst(topo, d) for d in out[core]], dma_engine_mask=e2[core],
                           remote_sem=T.sem["s%d" % l], srcs=tiles, dsts=[T["s%d" % l][:] for _ in out[core]],
                           alu_op=1)],
        local_sem=T.sem.sent)


def rank_program(g, core, T, topo):
    col, aid, out, src, d1, e1, e2, e3 = _plan(T, topo)
    S = T.sem
    rank = T.rank_of(core)
    if rank is None:
        for l in range(GC):
            if core in aid[l]:
                for k in range(GR):
                    g.wait_ge(S["q%d" % k], _bits(e1[col[l][k]]))
                _fold_and_send(g, T, topo, core, l, [T["pd%d" % k][:] for k in range(GR)], out, e2)
                g.wait_ge(S.sent, _bits(e2[core]))
        return
    RA, CB = T.tables["RA"], T.tables["CB"]
    assert all(v == row[0] for row in RA for v in row)
    i, j = rank // GC, rank % GC
    mates_on_chip = [k for k in range(GR) if k != i]

    g.sync.dma_start(T.xd[:], T.x[:]).then_inc(S.xl, 16)
    g.sync.dma_start(T.xs[:], T.x[:]).then_inc(S.xm, 16)
    g.sync.dma_start(T.aa[:], T.a[:]).then_inc(S.al, 16)

    g.wait_ge(S.xl, 16)
    if d1[core]:
        _copy(g, T, topo, T.xd[:], d1[core], "pd%d" % i, "q%d" % i, e1[core])
    if out[core]:
        for k in mates_on_chip:
            g.wait_ge(S["q%d" % k], _bits(e1[col[j][k]]))
        _fold_and_send(g, T, topo, core, j, [T.xd[:]] + [T["pd%d" % k][:] for k in mates_on_chip], out, e2)
    _copy(g, T, topo, T.xd[:], [col[j][k] for k in mates_on_chip], "p%d" % i, "p%d" % i, e3[core])
    g.wait_ge(S.sent, _bits(e1[core]) + _bits(e2[core]) + _bits(e3[core]))

    weight = [RA[i][0] * CB[j][l] for l in range(GC)]
    vals = sorted(set(w for w in weight if w != 1))
    lhs = {1: T.aa}
    for n, w in enumerate(vals):
        g.vector.memset(T["k%d" % n][:], float(w)).then_inc(S.cs, 1)
        lhs[w] = T["w%d" % n]
    if vals:
        g.vector.wait_ge(S.cs, len(vals))
    g.vector.wait_ge(S.al, 16)
    for n, w in enumerate(vals):
        g.vector.tensor_tensor(T["w%d" % n][:], T.aa[:], T["k%d" % n][:], AluOpType.mult).then_inc(S.sc, 1)

    g.tensor.wait_ge(S.al, 16)
    if vals:
        g.tensor.wait_ge(S.sc, len(vals))
    g.tensor.wait_ge(S.xm, 16)
    g.tensor.matmul(T.acc[:], lhs[weight[j]][:], T.xs[:], True, False)
    others = sorted((l for l in range(GC) if l != j), key=lambda l: len(aid[l]))
    for n, l in enumerate(others):
        if n == len(others) - 1:
            for k in mates_on_chip:
                g.tensor.wait_ge(S["p%d" % k], _bits(e3[col[j][k]]))
                g.tensor.matmul(T.acc[:], lhs[weight[j]][:], T["p%d" % k][:], False, False)
        g.tensor.wait_ge(S["s%d" % l], _bits(e2[src[(l, core)]]))
        mm = g.tensor.matmul(T.acc[:], lhs[weight[l]][:], T["s%d" % l][:], False, n == len(others) - 1)
    mm.then_inc(S.mm, 1)

    g.vector.wait_ge(S.mm, 1)
    g.vector.tensor_copy(T.ys[:], T.acc[:]).then_inc(S.cp, 1)
    g.sync.wait_ge(S.cp, 1)
    g.sync.dma_start(T.y[:], T.ys[:]).then_inc(S.st, 16)
    g.sync.wait_ge(S.st, 16)
